import numpy as np
import ml_dtypes


def mxq(x, axis, fmt="e4m3"):
    dtype, down = {"e4m3": (ml_dtypes.float8_e4m3fn, 7), "e5m2": (ml_dtypes.float8_e5m2, 14)}[fmt]
    v = np.moveaxis(np.asarray(x, np.float32).astype(ml_dtypes.bfloat16).astype(np.float64), axis, -1)
    blocks = v.reshape(v.shape[:-1] + (-1, 32))
    amax = np.abs(blocks).max(-1, keepdims=True)
    byte = np.maximum(np.where(amax > 0, np.frexp(amax)[1] - 1 + 127, 0) - down, 1)
    scale = np.exp2(byte - 127.0)
    codes = (blocks / scale).astype(np.float32).astype(dtype).astype(np.float64)
    return np.moveaxis((codes * scale).reshape(v.shape), -1, axis)


WIDE = False


def mx_kscale(k):
    if not WIDE:
        return np.ones(k)
    levels = np.array([10, -10, 5, -5, 0])
    if k % 512:
        return np.exp2(np.random.permutation(np.resize(levels, k // 32))).repeat(32)
    a = np.empty((k // 512, 16))
    for p in range(k // 512):
        a[p, :8] = np.random.permutation(np.resize(levels, 8))
        for g in range(8):
            far = levels[np.abs(levels - a[p, g]) >= 10]
            a[p, g + 8] = far[np.random.randint(len(far))]
    return np.exp2(a.ravel()).repeat(32)


def f64(x):
    return np.asarray(x).astype(np.float64)


def striped(idx):
    return np.tile(idx.reshape(-1, 16).T, (8, 1)).astype(np.uint16)


def unstriped(offs):
    return offs[:16].T.reshape(-1).astype(np.int64)


def pack_weight(w):
    k, n = w.shape
    w = f64(np.asarray(w, np.float32).astype(ml_dtypes.bfloat16)).reshape(k // 32, 32, n)
    amax = np.abs(w).max(1)
    byte = np.clip(np.where(amax > 0, np.frexp(amax)[1] - 1 + 127 - 7, 1), 1, 254)
    scaled = (w * np.exp2(127.0 - byte)[:, None, :]).reshape(k, n).astype(np.float32)
    words = np.ascontiguousarray(scaled.reshape(k // 512, 128, 4, n).transpose(0, 1, 3, 2)).astype(ml_dtypes.float8_e4m3fn).view(np.uint8)
    return words, np.ascontiguousarray(byte.astype(np.uint8).reshape(k // 512, 16, n))


def unpack_weight(words, scales):
    g, p, n, _ = words.shape
    vals = np.ascontiguousarray(words).view(ml_dtypes.float8_e4m3fn).astype(np.float64) * np.repeat(np.exp2(scales.astype(np.float64) - 127.0), 8, axis=1)[..., None]
    return vals.transpose(0, 1, 3, 2).reshape(g * 512, n)


def relu(v):
    return np.maximum(v, 0.0)


def sigmoid(v):
    return 1.0 / (1.0 + np.exp(-np.maximum(v, -700.0)))


K, T, S, V, N = 1024, 1024, 512, 256, 128


def setup_inputs():
    n = np.random.standard_normal
    s = mx_kscale(K)[:, None]
    packed_xT = pack_weight(n((K, T)) * s)
    return {
        "x_words": packed_xT[0],
        "x_scales": packed_xT[1],
        "w1": (n((K, N)) / np.sqrt(K) / s).astype(np.float32),
        "w2": (n((K, N)) / np.sqrt(K) / s).astype(np.float32),
        "w3": (n((K, N)) / np.sqrt(K) / s).astype(np.float32),
        "offs": striped(np.random.permutation(T)[:S]),
        "cen": striped(np.random.permutation(S)[:V]),
        "pos1": striped(np.random.permutation(S)[:V]),
        "pos2": striped(np.random.permutation(S)[:V]),
        "pos3": striped(np.random.permutation(S)[:V]),
    }


def reference(x_words, x_scales, w1, w2, w3, offs, cen, pos1, pos2, pos3):
    xq = unpack_weight(x_words, x_scales)[:, unstriped(offs)]
    y = mxq(f64(w1), 0, "e4m3").T @ xq
    yc = y[:, unstriped(cen)]
    e = mxq(f64(w2), 0, "e4m3").T @ xq
    h = mxq(f64(w3), 0, "e4m3").T @ xq
    z = (sigmoid(yc + e[:, unstriped(pos1)])) * h[:, unstriped(pos1)] + (sigmoid(yc + e[:, unstriped(pos2)])) * h[:, unstriped(pos2)] + (sigmoid(yc + e[:, unstriped(pos3)])) * h[:, unstriped(pos3)]
    return relu(z)

@@ -1,0 +1,168 @@
+from contextlib import ExitStack
+
+import concourse.mybir as mybir
+
+F32 = mybir.dt.float32
+BF16 = mybir.dt.bfloat16
+I32 = mybir.dt.int32
+U32 = mybir.dt.uint32
+U16 = mybir.dt.uint16
+U8 = mybir.dt.uint8
+FP8X4 = mybir.dt.float8_e4m3fn_x4
+ACT = mybir.ActivationFunctionType
+ALU = mybir.AluOpType
+
+K, T, S, V, N = 1024, 1024, 512, 256, 128
+P = 128
+PASSES = 2
+FLOPS = 3 * 2 * K * N * S
+
+
+def tile_picked_gatedg_relu_p_kernel(
+    tc, x_words, x_scales, w1, w2, w3, offs, cen, pos1, pos2, pos3, out
+):
+    nc = tc.nc
+    with ExitStack() as ctx:
+        sb = ctx.enter_context(tc.tile_pool(name="sb", bufs=1))
+        psum = ctx.enter_context(tc.psum_pool(name="psum", bufs=1))
+
+        def load_list(name, src):
+            t = sb.tile([P, src.shape[1]], U16, name=name)
+            nc.sync.dma_start(t[:], src)
+            return t
+
+        def load_words(z):
+            w = sb.tile([P, T], I32, name="word_window%d" % z, align_bytes=64)
+            nc.sync.dma_start(out=w[:], in_=x_words[z].rearrange("p n t -> p (n t)").bitcast(I32))
+            return w
+
+        def load_weight(name, w, z):
+            raw = sb.tile([P, 4, N], F32, name="%s_raw%d" % (name, z), tag="%s_raw%d" % (name, z))
+            nc.sync.dma_start(out=raw[:], in_=w[512 * z : 512 * (z + 1), :].rearrange("(p j) m -> p j m", j=4))
+            return raw
+
+        scale_window = sb.tile([P, T], U8, name="scale_window", align_bytes=64)
+        nc.vector.memset(scale_window[:].bitcast(I32), 0)
+        warm = sb.tile([P, 1], F32, name="warm")
+        nc.vector.memset(warm[:], 0.0)
+        warm_out = sb.tile([P, 1], F32, name="warm_out")
+        nc.scalar.activation(warm_out[:], warm[:], ACT.Sigmoid)
+
+        offs_t = load_list("offs_t", offs)
+        pos1_t = load_list("pos1_t", pos1)
+        for q in range(4):
+            nc.sync.dma_start(
+                out=scale_window[32 * q : 32 * q + 8, :].bitcast(I32),
+                in_=x_scales[:, 4 * q : 4 * q + 4, :].bitcast(I32),
+            )
+        win0 = load_words(0)
+        raw2a = load_weight("w2", w2, 0)
+        win1 = load_words(1)
+        raw2b = load_weight("w2", w2, 1)
+        pos2_t = load_list("pos2_t", pos2)
+        raw1a = load_weight("w1", w1, 0)
+        raw1b = load_weight("w1", w1, 1)
+        raw3a = load_weight("w3", w3, 0)
+        raw3b = load_weight("w3", w3, 1)
+        pos3_t = load_list("pos3_t", pos3)
+        cen_t = load_list("cen_t", cen)
+        pos = [pos1_t, pos2_t, pos3_t]
+
+        def gather_words(z, win):
+            g = sb.tile([P, S], U32, name="x_codes%d" % z, align_bytes=64)
+            nc.vector.tensor_copy(g[:], win[:].bitcast(U32).indirect(offs_t[:]))
+            return g
+
+        def interleave(name, raw, engine, tag):
+            grouped = sb.tile([P, N, 4], BF16, name=name + "_grouped", tag=tag, align_bytes=64)
+            src = raw[:].rearrange("p t (c i) -> p c t i", i=4)
+            dst = grouped[:].rearrange("p (c i) t -> p c t i", i=4)
+            if engine == "scalar":
+                nc.scalar.copy(dst, src)
+            else:
+                nc.vector.tensor_copy(dst, src)
+            return grouped
+
+        def quantise(name, grouped):
+            codes = sb.tile([P, N], U32, name=name + "_codes", align_bytes=64)
+            scales = sb.tile([P, N], U8, name=name + "_scales", align_bytes=64)
+            nc.vector.quantize_mx(
+                out=codes[:].bitcast(FP8X4), scales=scales[:], in_=grouped[:].rearrange("p m t -> p (m t)")
+            )
+            return codes, scales
+
+        def halves(name):
+            return [psum.tile([P, S // 2], F32, name="%s_acc%d" % (name, c)) for c in range(2)]
+
+        def multiply(accs, weight, z, codes):
+            for c in range(2):
+                cols = slice(c * S // 2, (c + 1) * S // 2)
+                nc.tensor.matmul_mx(
+                    out=accs[c][:],
+                    lhsT=weight[0][:].bitcast(FP8X4),
+                    lhsT_scale=weight[1][:],
+                    rhs=codes[:, cols].bitcast(FP8X4),
+                    rhs_scale=x_scale[4 * z : P, cols],
+                    start=(z == 0),
+                    stop=(z == PASSES - 1),
+                )
+
+        def evacuate(name, accs, tag):
+            res = sb.tile([P, S], F32, name=name, tag=tag)
+            for c in range(2):
+                nc.scalar.copy(res[:, c * S // 2 : (c + 1) * S // 2], accs[c][:])
+            return res
+
+        def gather(name, table, offsets, tag):
+            t = sb.tile([P, V], F32, name=name, tag=tag, align_bytes=64)
+            nc.vector.tensor_copy(t[:], table[:].indirect(offsets[:]))
+            return t
+
+        x_scale = sb.tile([P, S], U8, name="x_scale", align_bytes=64)
+        nc.vector.tensor_copy(x_scale[:], scale_window[:].indirect(offs_t[:]))
+        codes0 = gather_words(0, win0)
+        e_acc, y_acc, h_acc = halves("e"), halves("y"), halves("h")
+        g2a = interleave("w2a", raw2a, "scalar", "g2a")
+        multiply(e_acc, quantise("w2a", g2a), 0, codes0)
+        codes1 = gather_words(1, win1)
+        g2b = interleave("w2b", raw2b, "scalar", "g2b")
+        multiply(e_acc, quantise("w2b", g2b), 1, codes1)
+        e = evacuate("e", e_acc, "e")
+        g1a = interleave("w1a", raw1a, "vector", "g2b")
+        g1b = interleave("w1b", raw1b, "vector", "g1b")
+        multiply(y_acc, quantise("w1a", g1a), 0, codes0)
+        multiply(y_acc, quantise("w1b", g1b), 1, codes1)
+        g3a = interleave("w3a", raw3a, "scalar", "g3a")
+        g3b = interleave("w3b", raw3b, "scalar", "g3b")
+        y = evacuate("y", y_acc, "w3_raw1")
+        multiply(h_acc, quantise("w3a", g3a), 0, codes0)
+        multiply(h_acc, quantise("w3b", g3b), 1, codes1)
+        h = evacuate("h", h_acc, "h")
+
+        eg = []
+        eg.append(gather("eg0", e, pos[0], "g1b")[:])
+        eg.append(gather("eg1", e, pos[1], "g3a")[:])
+        pair = sb.tile([P, 2, V], F32, name="pair", tag="g3b", align_bytes=64)
+        nc.vector.tensor_copy(pair[:, 0, :], e[:].indirect(pos[2][:]))
+        nc.vector.tensor_copy(pair[:, 1, :], y[:].indirect(cen_t[:]))
+        eg.append(pair[:, 0, :])
+        yc = pair[:, 1, :]
+        terms = []
+        gates = []
+        for d in range(3):
+            u = sb.tile([P, V], F32, name="u%d" % d)
+            nc.vector.tensor_tensor(u[:], eg[d], yc, ALU.add)
+            s = sb.tile([P, V], F32, name="s%d" % d)
+            nc.scalar.activation(s[:], u[:], ACT.Sigmoid)
+            gates.append(s)
+        for d in range(3):
+            m = sb.tile([P, V], F32, name="m%d" % d)
+            nc.vector.tensor_tensor(m[:], h[:].indirect(pos[d][:]), gates[d][:], ALU.mult)
+            terms.append(m)
+        a = sb.tile([P, V], F32, name="a")
+        nc.vector.tensor_tensor(a[:], terms[0][:], terms[1][:], ALU.add)
+        b = sb.tile([P, V], F32, name="b")
+        nc.vector.tensor_tensor(b[:], a[:], terms[2][:], ALU.add)
+        r = sb.tile([P, V], F32, name="r")
+        nc.vector.tensor_scalar_max(r[:], b[:], 0.0)
+        nc.sync.dma_start(out=out, in_=r[:])

@@ -49,58 +49,59 @@ def tile_picked_gatedg_relu_p_kernel(
         nc.scalar.activation(warm_out[:], warm[:], ACT.Sigmoid)
 
         offs_t = load_list("offs_t", offs)
-        pos1_t = load_list("pos1_t", pos1)
+        win0 = load_words(0)
         for q in range(4):
             nc.sync.dma_start(
                 out=scale_window[32 * q : 32 * q + 8, :].bitcast(I32),
                 in_=x_scales[:, 4 * q : 4 * q + 4, :].bitcast(I32),
             )
-        win0 = load_words(0)
         raw2a = load_weight("w2", w2, 0)
-        win1 = load_words(1)
         raw2b = load_weight("w2", w2, 1)
-        pos2_t = load_list("pos2_t", pos2)
+        win1 = load_words(1)
         raw1a = load_weight("w1", w1, 0)
         raw1b = load_weight("w1", w1, 1)
         raw3a = load_weight("w3", w3, 0)
         raw3b = load_weight("w3", w3, 1)
-        pos3_t = load_list("pos3_t", pos3)
+        pos1_t = load_list("pos1_t", pos1)
+        pos2_t = load_list("pos2_t", pos2)
         cen_t = load_list("cen_t", cen)
+        pos3_t = load_list("pos3_t", pos3)
         pos = [pos1_t, pos2_t, pos3_t]
 
-        def gather_words(z, win):
+        def gather_words(z, win, pieces):
             g = sb.tile([P, S], U32, name="x_codes%d" % z, align_bytes=64)
-            nc.vector.tensor_copy(g[:], win[:].bitcast(U32).indirect(offs_t[:]))
+            for c in pieces:
+                nc.vector.tensor_copy(g[:, c], win[:].bitcast(U32).indirect(offs_t[:, c.start // 16 : c.stop // 16]))
             return g
 
-        def interleave(name, raw, engine, tag):
-            grouped = sb.tile([P, N, 4], BF16, name=name + "_grouped", tag=tag, align_bytes=64)
+        def group_tile(name, passes):
+            return sb.tile([P, passes, N, 4], BF16, name=name, align_bytes=64)
+
+        def interleave(raw, engine, grouped):
             src = raw[:].rearrange("p t (c i) -> p c t i", i=4)
-            dst = grouped[:].rearrange("p (c i) t -> p c t i", i=4)
+            dst = grouped.rearrange("p (c i) t -> p c t i", i=4)
             if engine == "scalar":
                 nc.scalar.copy(dst, src)
             else:
                 nc.vector.tensor_copy(dst, src)
             return grouped
 
-        def quantise(name, grouped):
-            codes = sb.tile([P, N], U32, name=name + "_codes", align_bytes=64)
-            scales = sb.tile([P, N], U8, name=name + "_scales", align_bytes=64)
-            nc.vector.quantize_mx(
-                out=codes[:].bitcast(FP8X4), scales=scales[:], in_=grouped[:].rearrange("p m t -> p (m t)")
-            )
+        def quantise(name, grouped, passes):
+            codes = sb.tile([P, passes * N], U32, name=name + "_codes", align_bytes=64)
+            scales = sb.tile([P, passes * N], U8, name=name + "_scales", align_bytes=64)
+            nc.vector.quantize_mx(out=codes[:].bitcast(FP8X4), scales=scales[:], in_=grouped.rearrange("p m t -> p (m t)"))
             return codes, scales
 
-        def halves(name):
-            return [psum.tile([P, S // 2], F32, name="%s_acc%d" % (name, c)) for c in range(2)]
+        def banks(name, pieces):
+            return [(c, psum.tile([P, c.stop - c.start], F32, name="%s_acc%d" % (name, c.start))) for c in pieces]
 
-        def multiply(accs, weight, z, codes):
-            for c in range(2):
-                cols = slice(c * S // 2, (c + 1) * S // 2)
+        def multiply(accs, weight, slot, z, codes):
+            m = slice(slot * N, (slot + 1) * N)
+            for cols, acc in accs:
                 nc.tensor.matmul_mx(
-                    out=accs[c][:],
-                    lhsT=weight[0][:].bitcast(FP8X4),
-                    lhsT_scale=weight[1][:],
+                    out=acc[:],
+                    lhsT=weight[0][:, m].bitcast(FP8X4),
+                    lhsT_scale=weight[1][:, m],
                     rhs=codes[:, cols].bitcast(FP8X4),
                     rhs_scale=x_scale[4 * z : P, cols],
                     start=(z == 0),
@@ -109,8 +110,8 @@ def tile_picked_gatedg_relu_p_kernel(
 
         def evacuate(name, accs, tag):
             res = sb.tile([P, S], F32, name=name, tag=tag)
-            for c in range(2):
-                nc.scalar.copy(res[:, c * S // 2 : (c + 1) * S // 2], accs[c][:])
+            for cols, acc in accs:
+                nc.scalar.copy(res[:, cols], acc[:])
             return res
 
         def gather(name, table, offsets, tag):
@@ -118,40 +119,41 @@ def tile_picked_gatedg_relu_p_kernel(
             nc.vector.tensor_copy(t[:], table[:].indirect(offsets[:]))
             return t
 
+        whole = [slice(0, S)]
+        halves = [slice(0, 256), slice(256, S)]
+        taper = [slice(0, 256), slice(256, 384), slice(384, S)]
+        codes0 = gather_words(0, win0, whole)
         x_scale = sb.tile([P, S], U8, name="x_scale", align_bytes=64)
         nc.vector.tensor_copy(x_scale[:], scale_window[:].indirect(offs_t[:]))
-        codes0 = gather_words(0, win0)
-        e_acc, y_acc, h_acc = halves("e"), halves("y"), halves("h")
-        g2a = interleave("w2a", raw2a, "scalar", "g2a")
-        multiply(e_acc, quantise("w2a", g2a), 0, codes0)
-        codes1 = gather_words(1, win1)
-        g2b = interleave("w2b", raw2b, "scalar", "g2b")
-        multiply(e_acc, quantise("w2b", g2b), 1, codes1)
-        e = evacuate("e", e_acc, "e")
-        g1a = interleave("w1a", raw1a, "vector", "g2b")
-        g1b = interleave("w1b", raw1b, "vector", "g1b")
-        multiply(y_acc, quantise("w1a", g1a), 0, codes0)
-        multiply(y_acc, quantise("w1b", g1b), 1, codes1)
-        g3a = interleave("w3a", raw3a, "scalar", "g3a")
-        g3b = interleave("w3b", raw3b, "scalar", "g3b")
+        e_acc, y_acc, h_acc = banks("e", taper), banks("y", halves), banks("h", halves)
+        g2a = interleave(raw2a, "scalar", group_tile("g2a", 1)[:, 0])
+        g2b = interleave(raw2b, "scalar", group_tile("g2b", 1)[:, 0])
+        multiply(e_acc, quantise("w2a", g2a, 1), 0, 0, codes0)
+        q2b = quantise("w2b", g2b, 1)
+        codes1 = gather_words(1, win1, taper)
+        multiply(e_acc, q2b, 0, 1, codes1)
+        g1a = interleave(raw1a, "scalar", group_tile("g1a", 1)[:, 0])
+        g1b = interleave(raw1b, "scalar", group_tile("g1b", 1)[:, 0])
+        e = evacuate("e", e_acc, "w1_raw1")
+        multiply(y_acc, quantise("w1a", g1a, 1), 0, 0, codes0)
+        g3a = interleave(raw3a, "vector", group_tile("g3a", 1)[:, 0])
+        multiply(y_acc, quantise("w1b", g1b, 1), 0, 1, codes1)
+        multiply(h_acc, quantise("w3a", g3a, 1), 0, 0, codes0)
+        g3b = interleave(raw3b, "scalar", group_tile("g3b", 1)[:, 0])
         y = evacuate("y", y_acc, "w3_raw1")
-        multiply(h_acc, quantise("w3a", g3a), 0, codes0)
-        multiply(h_acc, quantise("w3b", g3b), 1, codes1)
+        multiply(h_acc, quantise("w3b", g3b, 1), 0, 1, codes1)
         h = evacuate("h", h_acc, "h")
 
         eg = []
-        eg.append(gather("eg0", e, pos[0], "g1b")[:])
-        eg.append(gather("eg1", e, pos[1], "g3a")[:])
-        pair = sb.tile([P, 2, V], F32, name="pair", tag="g3b", align_bytes=64)
-        nc.vector.tensor_copy(pair[:, 0, :], e[:].indirect(pos[2][:]))
-        nc.vector.tensor_copy(pair[:, 1, :], y[:].indirect(cen_t[:]))
-        eg.append(pair[:, 0, :])
-        yc = pair[:, 1, :]
+        for d in range(2):
+            eg.append(gather("eg%d" % d, e, pos[d], "eg%d" % d))
+        yc = gather("yc", y, cen_t, "yc")
+        eg.append(gather("eg2", e, pos[2], "eg2"))
         terms = []
         gates = []
         for d in range(3):
             u = sb.tile([P, V], F32, name="u%d" % d)
-            nc.vector.tensor_tensor(u[:], eg[d], yc, ALU.add)
+            nc.vector.tensor_tensor(u[:], eg[d][:], yc[:], ALU.add)
             s = sb.tile([P, V], F32, name="s%d" % d)
             nc.scalar.activation(s[:], u[:], ACT.Sigmoid)
             gates.append(s)
@@ -159,10 +161,13 @@ def tile_picked_gatedg_relu_p_kernel(
             m = sb.tile([P, V], F32, name="m%d" % d)
             nc.vector.tensor_tensor(m[:], h[:].indirect(pos[d][:]), gates[d][:], ALU.mult)
             terms.append(m)
+        cols = [slice(0, V // 2), slice(V // 2, V)]
         a = sb.tile([P, V], F32, name="a")
         nc.vector.tensor_tensor(a[:], terms[0][:], terms[1][:], ALU.add)
-        b = sb.tile([P, V], F32, name="b")
-        nc.vector.tensor_tensor(b[:], a[:], terms[2][:], ALU.add)
-        r = sb.tile([P, V], F32, name="r")
-        nc.vector.tensor_scalar_max(r[:], b[:], 0.0)
-        nc.sync.dma_start(out=out, in_=r[:])
+        b = [sb.tile([P, V // 2], F32, name="b%d" % c) for c in range(2)]
+        r = [sb.tile([P, V // 2], F32, name="r%d" % c) for c in range(2)]
+        for c in range(2):
+            nc.vector.tensor_tensor(b[c][:], a[:, cols[c]], terms[2][:, cols[c]], ALU.add)
+        for c in range(2):
+            nc.vector.tensor_scalar_max(r[c][:], b[c][:], 0.0)
+            nc.sync.dma_start(out=out[:, cols[c]], in_=r[c][:])

@@ -1,6 +1,7 @@
 from contextlib import ExitStack
 
 import concourse.mybir as mybir
+from concourse.masks import make_identity
 
 F32 = mybir.dt.float32
 BF16 = mybir.dt.bfloat16
@@ -48,6 +49,8 @@ def tile_picked_gatedg_relu_p_kernel(
         warm_out = sb.tile([P, 1], F32, name="warm_out")
         nc.scalar.activation(warm_out[:], warm[:], ACT.Sigmoid)
 
+        ident = sb.tile([P, P], F32, name="ident")
+        make_identity(nc, ident[:])
         offs_t = load_list("offs_t", offs)
         win0 = load_words(0)
         for q in range(4):
@@ -61,10 +64,10 @@ def tile_picked_gatedg_relu_p_kernel(
         raw1a = load_weight("w1", w1, 0)
         raw1b = load_weight("w1", w1, 1)
         raw3a = load_weight("w3", w3, 0)
+        cen_t = load_list("cen_t", cen)
         raw3b = load_weight("w3", w3, 1)
         pos1_t = load_list("pos1_t", pos1)
         pos2_t = load_list("pos2_t", pos2)
-        cen_t = load_list("cen_t", cen)
         pos3_t = load_list("pos3_t", pos3)
         pos = [pos1_t, pos2_t, pos3_t]
 
@@ -93,7 +96,7 @@ def tile_picked_gatedg_relu_p_kernel(
             return codes, scales
 
         def banks(name, pieces):
-            return [(c, psum.tile([P, c.stop - c.start], F32, name="%s_acc%d" % (name, c.start))) for c in pieces]
+            return [(c, psum.tile([P, c.stop - c.start], F32, name="%s_acc%d" % (name, c.start), tag="%s_acc%d" % (name, c.start))) for c in pieces]
 
         def multiply(accs, weight, slot, z, codes):
             m = slice(slot * N, (slot + 1) * N)
@@ -149,25 +152,39 @@ def tile_picked_gatedg_relu_p_kernel(
             eg.append(gather("eg%d" % d, e, pos[d], "eg%d" % d))
         yc = gather("yc", y, cen_t, "yc")
         eg.append(gather("eg2", e, pos[2], "eg2"))
-        terms = []
-        gates = []
-        for d in range(3):
+        cols = [slice(0, V // 2), slice(V // 2, V)]
+        turned = [psum.tile([P, P], F32, name="turned%d" % c, tag="e_acc%d" % (0, 256)[c]) for c in range(2)]
+        for c in range(2):
+            nc.tensor.matmul(turned[c][:], lhsT=eg[0][:, cols[c]], rhs=ident[:], is_transpose=True, start=True, stop=False)
+        gate0 = psum.tile([P, V], F32, name="gate0", tag="e_acc384")
+        for c in range(2):
+            nc.tensor.matmul(turned[c][:], lhsT=yc[:, cols[c]], rhs=ident[:], is_transpose=True, start=False, stop=True)
+            st = sb.tile([P, P], F32, name="st%d" % c)
+            nc.scalar.activation(st[:], turned[c][:], ACT.Sigmoid)
+            nc.tensor.transpose(gate0[:, cols[c]], st[:], ident[:])
+        gates = {}
+        for d in (1, 2):
             u = sb.tile([P, V], F32, name="u%d" % d)
             nc.vector.tensor_tensor(u[:], eg[d][:], yc[:], ALU.add)
-            s = sb.tile([P, V], F32, name="s%d" % d)
+            s = sb.tile([P, V], F32, name="s%d" % d, tag="s%d" % d, align_bytes=64)
             nc.scalar.activation(s[:], u[:], ACT.Sigmoid)
-            gates.append(s)
-        for d in range(3):
+            gates[d] = s
+        hg0 = gather("hg0", h, pos[0], "eg1")
+        terms = {}
+        for d in (1, 2):
             m = sb.tile([P, V], F32, name="m%d" % d)
             nc.vector.tensor_tensor(m[:], h[:].indirect(pos[d][:]), gates[d][:], ALU.mult)
-            terms.append(m)
-        cols = [slice(0, V // 2), slice(V // 2, V)]
-        a = sb.tile([P, V], F32, name="a")
-        nc.vector.tensor_tensor(a[:], terms[0][:], terms[1][:], ALU.add)
+            terms[d] = m
+        m0 = sb.tile([P, V], F32, name="m0", tag="s1", align_bytes=64)
+        nc.vector.tensor_tensor(m0[:], hg0[:], gate0[:], ALU.mult)
+        terms[0] = m0
+        a = [sb.tile([P, V // 2], F32, name="a%d" % c) for c in range(2)]
+        for c in range(2):
+            nc.vector.tensor_tensor(a[c][:], terms[1][:, cols[c]], terms[2][:, cols[c]], ALU.add)
         b = [sb.tile([P, V // 2], F32, name="b%d" % c) for c in range(2)]
         r = [sb.tile([P, V // 2], F32, name="r%d" % c) for c in range(2)]
         for c in range(2):
-            nc.vector.tensor_tensor(b[c][:], a[:, cols[c]], terms[2][:, cols[c]], ALU.add)
+            nc.vector.tensor_tensor(b[c][:], a[c][:], terms[0][:, cols[c]], ALU.add)
         for c in range(2):
             nc.vector.tensor_scalar_max(r[c][:], b[c][:], 0.0)
             nc.sync.dma_start(out=out[:, cols[c]], in_=r[c][:])

from contextlib import ExitStack

import concourse.mybir as mybir
from concourse.masks import make_identity

F32 = mybir.dt.float32
BF16 = mybir.dt.bfloat16
I32 = mybir.dt.int32
U32 = mybir.dt.uint32
U16 = mybir.dt.uint16
U8 = mybir.dt.uint8
FP8X4 = mybir.dt.float8_e4m3fn_x4
ACT = mybir.ActivationFunctionType
ALU = mybir.AluOpType

K, T, S, V, N = 1024, 1024, 512, 256, 128
P = 128
PASSES = 2
FLOPS = 3 * 2 * K * N * S


def tile_picked_gatedg_relu_p_kernel(
    tc, x_words, x_scales, w1, w2, w3, offs, cen, pos1, pos2, pos3, out
):
    nc = tc.nc
    with ExitStack() as ctx:
        sb = ctx.enter_context(tc.tile_pool(name="sb", bufs=1))
        psum = ctx.enter_context(tc.psum_pool(name="psum", bufs=1))

        def load_list(name, src):
            t = sb.tile([P, src.shape[1]], U16, name=name)
            nc.sync.dma_start(t[:], src)
            return t

        def load_words(z):
            w = sb.tile([P, T], I32, name="word_window%d" % z, align_bytes=64)
            nc.sync.dma_start(out=w[:], in_=x_words[z].rearrange("p n t -> p (n t)").bitcast(I32))
            return w

        def load_weight(name, w, z):
            raw = sb.tile([P, 4, N], F32, name="%s_raw%d" % (name, z), tag="%s_raw%d" % (name, z))
            nc.sync.dma_start(out=raw[:], in_=w[512 * z : 512 * (z + 1), :].rearrange("(p j) m -> p j m", j=4))
            return raw

        scale_window = sb.tile([P, T], U8, name="scale_window", align_bytes=64)
        nc.vector.memset(scale_window[:].bitcast(I32), 0)
        warm = sb.tile([P, 1], F32, name="warm")
        nc.vector.memset(warm[:], 0.0)
        warm_out = sb.tile([P, 1], F32, name="warm_out")
        nc.scalar.activation(warm_out[:], warm[:], ACT.Sigmoid)

        ident = sb.tile([P, P], F32, name="ident")
        make_identity(nc, ident[:])
        offs_t = load_list("offs_t", offs)
        win0 = load_words(0)
        for q in range(4):
            nc.sync.dma_start(
                out=scale_window[32 * q : 32 * q + 8, :].bitcast(I32),
                in_=x_scales[:, 4 * q : 4 * q + 4, :].bitcast(I32),
            )
        raw2a = load_weight("w2", w2, 0)
        raw2b = load_weight("w2", w2, 1)
        win1 = load_words(1)
        raw1a = load_weight("w1", w1, 0)
        raw1b = load_weight("w1", w1, 1)
        raw3a = load_weight("w3", w3, 0)
        cen_t = load_list("cen_t", cen)
        raw3b = load_weight("w3", w3, 1)
        pos1_t = load_list("pos1_t", pos1)
        pos2_t = load_list("pos2_t", pos2)
        pos3_t = load_list("pos3_t", pos3)
        pos = [pos1_t, pos2_t, pos3_t]

        def gather_words(z, win, pieces):
            g = sb.tile([P, S], U32, name="x_codes%d" % z, align_bytes=64)
            for c in pieces:
                nc.vector.tensor_copy(g[:, c], win[:].bitcast(U32).indirect(offs_t[:, c.start // 16 : c.stop // 16]))
            return g

        def group_tile(name, passes):
            return sb.tile([P, passes, N, 4], BF16, name=name, align_bytes=64)

        def interleave(raw, engine, grouped):
            src = raw[:].rearrange("p t (c i) -> p c t i", i=4)
            dst = grouped.rearrange("p (c i) t -> p c t i", i=4)
            if engine == "scalar":
                nc.scalar.copy(dst, src)
            else:
                nc.vector.tensor_copy(dst, src)
            return grouped

        def quantise(name, grouped, passes):
            codes = sb.tile([P, passes * N], U32, name=name + "_codes", align_bytes=64)
            scales = sb.tile([P, passes * N], U8, name=name + "_scales", align_bytes=64)
            nc.vector.quantize_mx(out=codes[:].bitcast(FP8X4), scales=scales[:], in_=grouped.rearrange("p m t -> p (m t)"))
            return codes, scales

        def banks(name, pieces):
            return [(c, psum.tile([P, c.stop - c.start], F32, name="%s_acc%d" % (name, c.start), tag="%s_acc%d" % (name, c.start))) for c in pieces]

        def multiply(accs, weight, slot, z, codes):
            m = slice(slot * N, (slot + 1) * N)
            for cols, acc in accs:
                nc.tensor.matmul_mx(
                    out=acc[:],
                    lhsT=weight[0][:, m].bitcast(FP8X4),
                    lhsT_scale=weight[1][:, m],
                    rhs=codes[:, cols].bitcast(FP8X4),
                    rhs_scale=x_scale[4 * z : P, cols],
                    start=(z == 0),
                    stop=(z == PASSES - 1),
                )

        def evacuate(name, accs, tag):
            res = sb.tile([P, S], F32, name=name, tag=tag)
            for cols, acc in accs:
                nc.scalar.copy(res[:, cols], acc[:])
            return res

        def gather(name, table, offsets, tag):
            t = sb.tile([P, V], F32, name=name, tag=tag, align_bytes=64)
            nc.vector.tensor_copy(t[:], table[:].indirect(offsets[:]))
            return t

        whole = [slice(0, S)]
        halves = [slice(0, 256), slice(256, S)]
        taper = [slice(0, 256), slice(256, 384), slice(384, S)]
        codes0 = gather_words(0, win0, whole)
        x_scale = sb.tile([P, S], U8, name="x_scale", align_bytes=64)
        nc.vector.tensor_copy(x_scale[:], scale_window[:].indirect(offs_t[:]))
        e_acc, y_acc, h_acc = banks("e", taper), banks("y", halves), banks("h", halves)
        g2a = interleave(raw2a, "scalar", group_tile("g2a", 1)[:, 0])
        g2b = interleave(raw2b, "scalar", group_tile("g2b", 1)[:, 0])
        multiply(e_acc, quantise("w2a", g2a, 1), 0, 0, codes0)
        q2b = quantise("w2b", g2b, 1)
        codes1 = gather_words(1, win1, taper)
        multiply(e_acc, q2b, 0, 1, codes1)
        g1a = interleave(raw1a, "scalar", group_tile("g1a", 1)[:, 0])
        g1b = interleave(raw1b, "scalar", group_tile("g1b", 1)[:, 0])
        e = evacuate("e", e_acc, "w1_raw1")
        multiply(y_acc, quantise("w1a", g1a, 1), 0, 0, codes0)
        g3a = interleave(raw3a, "vector", group_tile("g3a", 1)[:, 0])
        multiply(y_acc, quantise("w1b", g1b, 1), 0, 1, codes1)
        multiply(h_acc, quantise("w3a", g3a, 1), 0, 0, codes0)
        g3b = interleave(raw3b, "scalar", group_tile("g3b", 1)[:, 0])
        y = evacuate("y", y_acc, "w3_raw1")
        multiply(h_acc, quantise("w3b", g3b, 1), 0, 1, codes1)
        h = evacuate("h", h_acc, "h")

        eg = []
        for d in range(2):
            eg.append(gather("eg%d" % d, e, pos[d], "eg%d" % d))
        yc = gather("yc", y, cen_t, "yc")
        eg.append(gather("eg2", e, pos[2], "eg2"))
        cols = [slice(0, V // 2), slice(V // 2, V)]
        turned = [psum.tile([P, P], F32, name="turned%d" % c, tag="e_acc%d" % (0, 256)[c]) for c in range(2)]
        for c in range(2):
            nc.tensor.matmul(turned[c][:], lhsT=eg[0][:, cols[c]], rhs=ident[:], is_transpose=True, start=True, stop=False)
        gate0 = psum.tile([P, V], F32, name="gate0", tag="e_acc384")
        for c in range(2):
            nc.tensor.matmul(turned[c][:], lhsT=yc[:, cols[c]], rhs=ident[:], is_transpose=True, start=False, stop=True)
            st = sb.tile([P, P], F32, name="st%d" % c)
            nc.scalar.activation(st[:], turned[c][:], ACT.Sigmoid)
            nc.tensor.transpose(gate0[:, cols[c]], st[:], ident[:])
        gates = {}
        for d in (1, 2):
            u = sb.tile([P, V], F32, name="u%d" % d)
            nc.vector.tensor_tensor(u[:], eg[d][:], yc[:], ALU.add)
            s = sb.tile([P, V], F32, name="s%d" % d, tag="s%d" % d, align_bytes=64)
            nc.scalar.activation(s[:], u[:], ACT.Sigmoid)
            gates[d] = s
        hg0 = gather("hg0", h, pos[0], "eg1")
        terms = {}
        for d in (1, 2):
            m = sb.tile([P, V], F32, name="m%d" % d)
            nc.vector.tensor_tensor(m[:], h[:].indirect(pos[d][:]), gates[d][:], ALU.mult)
            terms[d] = m
        m0 = sb.tile([P, V], F32, name="m0", tag="s1", align_bytes=64)
        nc.vector.tensor_tensor(m0[:], hg0[:], gate0[:], ALU.mult)
        terms[0] = m0
        a = [sb.tile([P, V // 2], F32, name="a%d" % c) for c in range(2)]
        for c in range(2):
            nc.vector.tensor_tensor(a[c][:], terms[1][:, cols[c]], terms[2][:, cols[c]], ALU.add)
        b = [sb.tile([P, V // 2], F32, name="b%d" % c) for c in range(2)]
        r = [sb.tile([P, V // 2], F32, name="r%d" % c) for c in range(2)]
        for c in range(2):
            nc.vector.tensor_tensor(b[c][:], a[c][:], terms[0][:, cols[c]], ALU.add)
        for c in range(2):
            nc.vector.tensor_scalar_max(r[c][:], b[c][:], 0.0)
            nc.sync.dma_start(out=out[:, cols[c]], in_=r[c][:])
